import numpy as np
import ml_dtypes


def mxq(x, axis, fmt="e4m3"):
    dtype, down = {"e4m3": (ml_dtypes.float8_e4m3fn, 7), "e5m2": (ml_dtypes.float8_e5m2, 14)}[fmt]
    v = np.moveaxis(np.asarray(x, np.float32).astype(ml_dtypes.bfloat16).astype(np.float64), axis, -1)
    blocks = v.reshape(v.shape[:-1] + (-1, 32))
    amax = np.abs(blocks).max(-1, keepdims=True)
    byte = np.maximum(np.where(amax > 0, np.frexp(amax)[1] - 1 + 127, 0) - down, 1)
    scale = np.exp2(byte - 127.0)
    codes = (blocks / scale).astype(np.float32).astype(dtype).astype(np.float64)
    return np.moveaxis((codes * scale).reshape(v.shape), -1, axis)


WIDE = False


def mx_kscale(k):
    if not WIDE:
        return np.ones(k)
    levels = np.array([10, -10, 5, -5, 0])
    if k % 512:
        return np.exp2(np.random.permutation(np.resize(levels, k // 32))).repeat(32)
    a = np.empty((k // 512, 16))
    for p in range(k // 512):
        a[p, :8] = np.random.permutation(np.resize(levels, 8))
        for g in range(8):
            far = levels[np.abs(levels - a[p, g]) >= 10]
            a[p, g + 8] = far[np.random.randint(len(far))]
    return np.exp2(a.ravel()).repeat(32)


def f64(x):
    return np.asarray(x).astype(np.float64)


def striped(idx):
    return np.tile(idx.reshape(-1, 16).T, (8, 1)).astype(np.uint16)


def unstriped(offs):
    return offs[:16].T.reshape(-1).astype(np.int64)


E2M1 = np.array([0.0, 0.5, 1.0, 1.5, 2.0, 3.0, 4.0, 6.0, -0.0, -0.5, -1.0, -1.5, -2.0, -3.0, -4.0, -6.0])


def pack_weight(w, fmt):
    k, n = w.shape
    w = f64(np.asarray(w, np.float32).astype(ml_dtypes.bfloat16)).reshape(k // 32, 32, n)
    amax = np.abs(w).max(1)
    if fmt == "e4m3":
        byte = np.frexp(amax)[1] - 1 + 127 - 7
    else:
        mant, ex = np.frexp(amax / 6.0)
        byte = np.where(mant > 0.5, ex, ex - 1) + 127
    byte = np.clip(np.where(amax > 0, byte, 1), 1, 254)
    scaled = (w * np.exp2(127.0 - byte)[:, None, :]).reshape(k, n).astype(np.float32)
    by_word = np.ascontiguousarray(scaled.reshape(k // 512, 128, 4, n).transpose(0, 1, 3, 2))
    if fmt == "e4m3":
        words = by_word.astype(ml_dtypes.float8_e4m3fn).view(np.uint8)
    else:
        c = by_word.astype(ml_dtypes.float4_e2m1fn).view(np.uint8) & 0xF
        words = (c[..., 0::2] | (c[..., 1::2] << 4)).reshape(k // 512, 128, 2 * n)
    return np.ascontiguousarray(words), np.ascontiguousarray(byte.astype(np.uint8).reshape(k // 512, 16, n))


def unpack_weight(words, scales, fmt):
    g, _, n = scales.shape
    words = np.ascontiguousarray(words).reshape(g, 128, n, -1)
    if fmt == "e4m3":
        vals = words.view(ml_dtypes.float8_e4m3fn).astype(np.float64)
    else:
        nib = np.empty((g, 128, n, 4), np.uint8)
        nib[..., 0::2] = words & 0xF
        nib[..., 1::2] = words >> 4
        vals = E2M1[nib]
    vals = vals * np.repeat(np.exp2(scales.astype(np.float64) - 127.0), 8, axis=1)[..., None]
    return vals.transpose(0, 1, 3, 2).reshape(g * 512, n)


def gelu(v):
    return 0.5 * v * (1.0 + np.tanh(np.sqrt(2.0 / np.pi) * (v + 0.044715 * v**3)))


def striped8(idx):
    return np.concatenate([v.reshape(-1, 16).T for v in idx]).astype(np.uint16)


def unstriped8(offs):
    return np.stack([offs[16 * g:16 * g + 16].T.reshape(-1) for g in range(8)]).astype(np.int64)


def heads(h, wgt, idx8):
    r = np.arange(h.shape[0])
    return wgt[r // 4 % 128] * h[r[:, None], idx8[r % 512 // 64]]


K, H, T, S, P = 512, 1024, 4096, 1024, 512

def setup_inputs():
    n = np.random.standard_normal
    s = mx_kscale(K)[:, None]
    u = mx_kscale(H)[:, None]
    tab_words, tab_scales = pack_weight(n((K, T)) * s, "e4m3")
    wf_words, wf_scales = pack_weight(n((K, H)) / np.sqrt(K) / s, "e2m1")
    return {
        "tab_words": tab_words, "tab_scales": tab_scales,
        "offs": striped(np.random.permutation(T)[:S]),
        "offs2": striped8(np.stack([np.random.permutation(S)[:P] for _ in range(8)])),
        "offs3": striped8(np.stack([np.random.permutation(S)[:P] for _ in range(8)])),
        "wm": (n((K, H)) / np.sqrt(K) / s).astype(np.float32),
        "bm": (0.6 * n(H)).astype(np.float32),
        "wf_words": wf_words, "wf_scales": wf_scales,
        "wga": np.repeat(np.random.uniform(0.5, 2.0, (8, P)), 16, axis=0).astype(np.float32),
        "wgb": np.repeat(np.random.uniform(0.5, 2.0, (8, P)), 16, axis=0).astype(np.float32),
        "gain": (np.exp(0.4 * n(H)) * u[:, 0]).astype(np.float32),
        "w3": (1.6 * n((H, H)) / np.sqrt(H) / u).astype(np.float32),
        "b3": (0.6 * n(H)).astype(np.float32),
    }

def reference(tab_words, tab_scales, offs, offs2, offs3, wm, bm, wf_words, wf_scales, wga, wgb, gain, w3, b3):
    v = unpack_weight(tab_words, tab_scales, "e4m3")[:, unstriped(offs)]
    hm = (mxq(f64(wm), 0, "e4m3").T @ v) + f64(bm)[:, None]
    hf = unpack_weight(wf_words, wf_scales, "e2m1").T @ v
    xa = heads(hm, f64(wga), unstriped8(offs2))
    xb = heads(hf, f64(wgb), unstriped8(offs3))
    z = f64(gain)[:, None] * np.tanh(xa * xb)
    y = (mxq(f64(w3), 0, "e4m3").T @ mxq(z, 0, "e4m3")) + f64(b3)[:, None]
    return np.maximum(y, xb)

from contextlib import ExitStack

import concourse.mybir as mybir

K, H, T, S, M = 512, 1024, 4096, 1024, 512
FLOPS = 2 * K * H * S * 2 + 2 * H * H * M

F32 = mybir.dt.float32
BF16 = mybir.dt.bfloat16
I32 = mybir.dt.int32
U32 = mybir.dt.uint32
U16 = mybir.dt.uint16
U8 = mybir.dt.uint8
FP8X4 = mybir.dt.float8_e4m3fn_x4
FP4X4 = mybir.dt.float4_e2m1fn_x4
ALU = mybir.AluOpType
ACT = mybir.ActivationFunctionType

P = 128
PACK = 4
PASS = P * PACK
BLOCKS = H // PASS
BANK = 512
H_BUFS = 10


def tile_list_pairbond_trip_scores_kernel(
    tc, tab_words, tab_scales, offs, offs2, offs3, wm, bm, wf_words, wf_scales, wga, wgb, gain, w3, b3, out
):
    nc = tc.nc
    with ExitStack() as ctx:
        lists = ctx.enter_context(tc.tile_pool(name="lists", bufs=1))
        keep = ctx.enter_context(tc.tile_pool(name="keep", bufs=1))
        ring = ctx.enter_context(tc.tile_pool(name="ring", bufs=2))
        hpool = ctx.enter_context(tc.tile_pool(name="hpool", bufs=H_BUFS))
        psum = ctx.enter_context(tc.psum_pool(name="psum", bufs=8))

        idx = lists.tile([P, S // 16], U16, name="idx")
        idx2 = lists.tile([P, M // 16], U16, name="idx2")
        idx3 = lists.tile([P, M // 16], U16, name="idx3")

        table = keep.tile([P, T], U32, name="table", tag="slot_table")
        table_sc = keep.tile([P, T], U8, name="table_sc", tag="slot_a", align_bytes=64)
        wf_raw = keep.tile([P, 2 * H], U8, name="wf_raw", tag="slot_b")
        wf_sc_raw = keep.tile([P, H], U8, name="wf_sc_raw", tag="slot_c", align_bytes=64)
        bm_sb = keep.tile([P, BLOCKS, PACK], F32, name="bm_sb")
        gain_sb = keep.tile([P, BLOCKS, PACK], F32, name="gain_sb")
        b3_sb = keep.tile([P, BLOCKS, PACK], F32, name="b3_sb")

        def load_scale_rows(tile, rows, queues):
            nc.vector.memset(tile[:].bitcast(I32), 0)
            for q in range(4):
                queues[q].dma_start(out=tile[32 * q : 32 * q + 4, :].bitcast(I32), in_=rows[4 * q : 4 * q + 4, :].bitcast(I32))

        def load_channel_vector(tile, vec):
            nc.sync.dma_start(out=tile[:], in_=vec.rearrange("(b p i) -> p b i", p=P, i=PACK))

        def load_weight(w, a, b, raw):
            rows = w[PASS * a : PASS * (a + 1), PASS * b : PASS * (b + 1)]
            nc.sync.dma_start(out=raw, in_=rows.rearrange("(p j) c -> p j c", j=PACK))
            return raw

        nc.sync.dma_start(idx[:], offs)
        nc.sync.dma_start(idx3[:], offs3)
        nc.sync.dma_start(idx2[:], offs2)
        load_channel_vector(bm_sb, bm)
        load_channel_vector(gain_sb, gain)
        load_channel_vector(b3_sb, b3)
        nc.sync.dma_start(out=wf_raw[:].bitcast(I32), in_=wf_words[0].bitcast(I32))
        nc.sync.dma_start(out=table[:].bitcast(I32), in_=tab_words[0].rearrange("p t i -> p (t i)").bitcast(I32))
        load_scale_rows(wf_sc_raw, wf_scales[0], [nc.gpsimd, nc.scalar, nc.scalar, nc.scalar])
        load_scale_rows(table_sc, tab_scales[0], [nc.scalar] * 4)

        def weight_slot(tag, name):
            return keep.tile([P, PACK, PASS], F32, name=name, tag=tag, align_bytes=64)[:]

        def deal_wf(b):
            words = keep.tile([P, 2 * PASS], U8, name=f"wf_words{b}", align_bytes=64)
            scales = keep.tile([P, PASS], U8, name=f"wf_scales{b}", align_bytes=64)
            nc.vector.tensor_copy(
                out=words[:].rearrange("p (i q e) -> p i q e", i=PACK, e=2),
                in_=wf_raw[:, 2 * PASS * b : 2 * PASS * (b + 1)].rearrange("p (q i e) -> p i q e", i=PACK, e=2),
            )
            nc.vector.tensor_copy(
                out=scales[:].rearrange("p (i q) -> p i q", i=PACK),
                in_=wf_sc_raw[:, PASS * b : PASS * (b + 1)].rearrange("p (q i) -> p i q", i=PACK),
            )
            return [(words[:, 2 * P * i : 2 * P * (i + 1)].bitcast(FP4X4), scales[:, P * i : P * (i + 1)]) for i in range(PACK)]

        def round_weight(raw, copy):
            rounded = ring.tile([P, PACK * PASS], BF16, name="rounded", align_bytes=64, bufs=3)
            copy(
                out=rounded[:].rearrange("p (i q j) -> p q i j", i=PACK, j=PACK),
                in_=raw.rearrange("p j (q i) -> p q i j", i=PACK),
            )
            return rounded

        def quantise(rounded, name):
            codes = keep.tile([P, PASS], U32, name=name + "_codes", align_bytes=64)
            scales = keep.tile([P, PASS], U8, name=name + "_scales", align_bytes=64)
            nc.vector.quantize_mx(out=codes[:].bitcast(FP8X4), scales=scales[:], in_=rounded[:])
            return codes, scales

        def stationary(quantised):
            codes, scales = quantised
            return [(codes[:, P * i : P * (i + 1)].bitcast(FP8X4), scales[:, P * i : P * (i + 1)]) for i in range(PACK)]

        wf_q = [deal_wf(b) for b in range(BLOCKS)]
        place_weights = keep.tile([P, 2, M], F32, name="place_weights", tag="slot_b")
        wgb_sb, wga_sb = place_weights[:, 0], place_weights[:, 1]
        nc.scalar.dma_start(out=wgb_sb, in_=wgb)
        nc.sync.dma_start(out=wga_sb, in_=wga)
        wm_raw = [load_weight(wm, 0, 0, weight_slot("slot_c", "wm_raw0"))]
        picked_sc = keep.tile([P, S], U8, name="picked_sc", tag="slot_d", align_bytes=64)
        nc.vector.tensor_copy(out=picked_sc[:], in_=table_sc[:].indirect(idx[:]))
        picked = keep.tile([P, S], U32, name="picked", tag="slot_a", align_bytes=64)
        for u in range(S // BANK):
            nc.vector.tensor_copy(
                out=picked[:, BANK * u : BANK * (u + 1)], in_=table[:].indirect(idx[:, BANK // 16 * u : BANK // 16 * (u + 1)])
            )
        after_table = keep.tile([P, 2, PACK, PASS], F32, name="after_table", tag="slot_table")
        wm_raw.append(load_weight(wm, 0, 1, after_table[:, 0]))
        w3_raw = {(0, 0): load_weight(w3, 0, 0, after_table[:, 1])}

        def features(weight, bias):
            h = hpool.tile([P, S], F32, name="h")
            for u in range(S // BANK):
                cols = slice(BANK * u, BANK * (u + 1))
                acc = psum.tile([P, BANK], F32, name="acc")
                nc.tensor.matmul_mx(
                    out=acc[:], lhsT=weight[0], lhsT_scale=weight[1],
                    rhs=picked[:, cols].bitcast(FP8X4), rhs_scale=picked_sc[:, cols], start=True, stop=True,
                )
                if bias is None:
                    nc.scalar.copy(out=h[:, cols], in_=acc[:])
                else:
                    nc.scalar.activation(out=h[:, cols], in_=acc[:], func=ACT.Identity, bias=bias)
            return h

        def pick(x, hs, offsets, weights):
            for i in range(PACK):
                nc.vector.tensor_tensor(out=x[:, i, :], in0=hs[i][:].indirect(offsets[:]), in1=weights, op=ALU.mult)

        def bound(agree):
            bounded = ring.tile([P, M, PACK], F32, name="bounded")
            nc.scalar.activation(out=bounded[:], in_=agree[:].rearrange("p i m -> p m i"), func=ACT.Tanh)
            return bounded

        def quantise_z(bounded, b):
            z = ring.tile([P, M * PACK], BF16, name="z", align_bytes=64)
            nc.vector.tensor_tensor(
                out=z[:].rearrange("p (m i) -> p m i", i=PACK), in0=bounded[:],
                in1=gain_sb[:, b, :].unsqueeze(1).to_broadcast([P, M, PACK]), op=ALU.mult,
            )
            return quantise(z, f"z{b}")

        xb = [keep.tile([P, PACK, M], F32, name=f"xb{b}") for b in range(BLOCKS)]
        xa = [keep.tile([P, PACK, M], F32, name=f"xa{b}") for b in range(BLOCKS)]

        def male(b, wm_q):
            return [features(wm_q[i], bm_sb[:, b, i : i + 1]) for i in range(PACK)]

        def female(b):
            return [features(wf_q[b][i], None) for i in range(PACK)]

        def multiply(b):
            nc.vector.tensor_tensor(out=xa[b][:], in0=xa[b][:], in1=xb[b][:], op=ALU.mult)

        hf = female(0)
        wm_q = stationary(quantise(round_weight(wm_raw[0], nc.vector.tensor_copy), "wm0"))
        w3_raw[1, 0] = load_weight(w3, 1, 0, weight_slot("slot_c", "w3_raw10"))
        pick(xb[0], hf, idx3, wgb_sb)
        hm = male(0, wm_q)
        pick(xa[0], hm, idx2, wga_sb)
        wm_q = stationary(quantise(round_weight(wm_raw[1], nc.scalar.copy), "wm1"))
        multiply(0)
        hf = female(1)
        pick(xb[1], hf, idx3, wgb_sb)
        hm = male(1, wm_q)
        w3_raw[0, 1] = load_weight(w3, 0, 1, weight_slot("slot_a", "w3_raw01"))
        w3_raw[1, 1] = load_weight(w3, 1, 1, weight_slot("slot_d", "w3_raw11"))
        bounded0 = bound(xa[0])
        pick(xa[1], hm, idx2, wga_sb)
        multiply(1)
        z_q = [quantise_z(bounded0, 0)]
        w3_q = {(0, 0): stationary(quantise(round_weight(w3_raw[0, 0], nc.scalar.copy), "w3_00"))}
        z_q.append(quantise_z(bound(xa[1]), 1))
        w3_q[1, 0] = stationary(quantise(round_weight(w3_raw[1, 0], nc.scalar.copy), "w3_10"))

        def scores(b):
            result = keep.tile([P, PACK, M], F32, name=f"result{b}")
            rows = out[PASS * b : PASS * (b + 1), :].rearrange("(p i) m -> p i m", i=PACK)
            accs = [psum.tile([P, M], F32, name="acc") for i in range(PACK)]
            for a in range(BLOCKS):
                for i in range(PACK):
                    nc.tensor.matmul_mx(
                        out=accs[i][:], lhsT=w3_q[a, b][i][0], lhsT_scale=w3_q[a, b][i][1],
                        rhs=z_q[a][0][:].bitcast(FP8X4), rhs_scale=z_q[a][1][:], start=(a == 0), stop=(a == BLOCKS - 1),
                    )
            for i in range(PACK):
                nc.vector.scalar_tensor_tensor(
                    out=result[:, i, :], in0=accs[i][:], scalar=b3_sb[:, b, i : i + 1], in1=xb[b][:, i, :],
                    op0=ALU.add, op1=ALU.max,
                )
                nc.sync.dma_start(out=rows[:, i, :], in_=result[:, i, :])

        rounded01 = round_weight(w3_raw[0, 1], nc.scalar.copy)
        scores(0)
        w3_q[0, 1] = stationary(quantise(rounded01, "w3_01"))
        w3_q[1, 1] = stationary(quantise(round_weight(w3_raw[1, 1], nc.scalar.copy), "w3_11"))
        scores(1)
